import numpy as np
import ml_dtypes


def mxq(x, axis, fmt="e4m3"):
    dtype, down = {"e4m3": (ml_dtypes.float8_e4m3fn, 7), "e5m2": (ml_dtypes.float8_e5m2, 14)}[fmt]
    v = np.moveaxis(np.asarray(x, np.float32).astype(ml_dtypes.bfloat16).astype(np.float64), axis, -1)
    blocks = v.reshape(v.shape[:-1] + (-1, 32))
    amax = np.abs(blocks).max(-1, keepdims=True)
    byte = np.maximum(np.where(amax > 0, np.frexp(amax)[1] - 1 + 127, 0) - down, 1)
    scale = np.exp2(byte - 127.0)
    codes = (blocks / scale).astype(np.float32).astype(dtype).astype(np.float64)
    return np.moveaxis((codes * scale).reshape(v.shape), -1, axis)


WIDE = False


def mx_kscale(k):
    if not WIDE:
        return np.ones(k)
    levels = np.array([10, -10, 5, -5, 0])
    if k % 512:
        return np.exp2(np.random.permutation(np.resize(levels, k // 32))).repeat(32)
    a = np.empty((k // 512, 16))
    for p in range(k // 512):
        a[p, :8] = np.random.permutation(np.resize(levels, 8))
        for g in range(8):
            far = levels[np.abs(levels - a[p, g]) >= 10]
            a[p, g + 8] = far[np.random.randint(len(far))]
    return np.exp2(a.ravel()).repeat(32)


def f64(x):
    return np.asarray(x).astype(np.float64)


def striped(idx):
    return np.tile(idx.reshape(-1, 16).T, (8, 1)).astype(np.uint16)


def unstriped(offs):
    return offs[:16].T.reshape(-1).astype(np.int64)


def striped8(idx):
    return np.concatenate([x.reshape(-1, 16).T for x in idx]).astype(np.uint16)


def runs(offs, k):
    lists = np.stack([offs[16 * r : 16 * r + 16].T.reshape(-1) for r in range(8)]).astype(np.int64)
    return lists[np.arange(k) % 512 // 64]


def pack_weight(w):
    k, n = w.shape
    w = f64(np.asarray(w, np.float32).astype(ml_dtypes.bfloat16)).reshape(k // 32, 32, n)
    amax = np.abs(w).max(1)
    byte = np.clip(np.where(amax > 0, np.frexp(amax)[1] - 1 + 127 - 7, 1), 1, 254)
    scaled = (w * np.exp2(127.0 - byte)[:, None, :]).reshape(k, n).astype(np.float32)
    words = np.ascontiguousarray(scaled.reshape(k // 512, 128, 4, n).transpose(0, 1, 3, 2)).astype(ml_dtypes.float8_e4m3fn).view(np.uint8)
    return words, np.ascontiguousarray(byte.astype(np.uint8).reshape(k // 512, 16, n))


def unpack_weight(words, scales):
    g, p, n, _ = words.shape
    vals = np.ascontiguousarray(words).view(ml_dtypes.float8_e4m3fn).astype(np.float64) * np.repeat(np.exp2(scales.astype(np.float64) - 127.0), 8, axis=1)[..., None]
    return vals.transpose(0, 1, 3, 2).reshape(g * 512, n)

def planes(y):
    n, m = y.shape
    v = y.astype(np.float32).astype(ml_dtypes.bfloat16).astype(np.float64).reshape(n // 32, 32, m)
    top = np.abs(v).max(1)
    byte = np.clip(np.where(top > 0, np.frexp(top)[1] - 1 + 127 - 7, 1), 1, 254)
    codes = (v * np.exp2(127.0 - byte)[:, None, :]).reshape(n, m).astype(np.float32).astype(ml_dtypes.float8_e4m3fn).view(np.uint8)
    words = codes.reshape(n // 512, 128, 4, m).transpose(0, 1, 3, 2)
    return np.ascontiguousarray(words), np.ascontiguousarray(byte.astype(np.uint8).reshape(n // 512, 16, m))


K, T, S, N, H, G, W, U = 512, 1024, 256, 512, 512, 2048, 1024, 192


def setup_inputs():
    n = np.random.standard_normal
    s = mx_kscale(K)[:, None]
    u = mx_kscale(K)
    packed_xT = pack_weight(n((K, T)) * s)
    packed_w1 = pack_weight(n((K, H)) / np.sqrt(K) / s)
    packed_dT = pack_weight(n((K, G)) / s)
    packed_w2 = pack_weight(n((H, N)) / np.sqrt(2 * H) / u[:, None])
    packed_w3 = pack_weight(n((H, N)) / np.sqrt(2 * H) / u[:, None])
    return {
        "x_words": packed_xT[0],
        "x_scales": packed_xT[1],
        "w1_words": packed_w1[0],
        "w1_scales": packed_w1[1],
        "d_words": packed_dT[0],
        "d_scales": packed_dT[1],
        "tau": np.random.uniform(0.3, 0.9, (H, 1)).astype(np.float32),
        "tau2": np.random.uniform(0.3, 0.9, (H, 1)).astype(np.float32),
        "gn": (np.random.uniform(0.5, 1.5, (H, 1)) * u[:, None]).astype(np.float32),
        "gk": (np.random.uniform(0.5, 1.5, (H, 1)) * u[:, None]).astype(np.float32),
        "w2_words": packed_w2[0],
        "w2_scales": packed_w2[1],
        "w3_words": packed_w3[0],
        "w3_scales": packed_w3[1],
        "offs": striped(np.random.permutation(T)[:S]),
        "kidx": striped8(np.random.randint(0, G, (8, H))),
        "two": striped(np.random.permutation(T)[:S]),
        "n1": striped(np.random.randint(0, S, W)),
        "n2": striped(np.random.permutation(S)),
        "n3": striped(np.random.permutation(S)),
        "n4": striped(np.random.permutation(S)[:U]),
        "n5": striped(np.random.permutation(S)[:U]),
    }


def reference(x_words, x_scales, w1_words, w1_scales, d_words, d_scales, tau, tau2, gn, gk, w2_words, w2_scales, w3_words, w3_scales, offs, kidx, two, n1, n2, n3, n4, n5):
    xq = unpack_weight(x_words, x_scales)[:, unstriped(offs)]
    y = unpack_weight(w1_words, w1_scales).T @ xq
    top = y.max(axis=1, keepdims=True)
    ea = np.exp(f64(tau) * (y[:, unstriped(n1)] - top))
    ms = ea.reshape(H, S, 4).sum(axis=2)
    z = f64(gn) * (np.log(ms + 0.25) - (0.5 * y))
    d_kidx = unpack_weight(d_words, d_scales)[np.arange(K)[:, None], runs(kidx, K)]
    x_two = unpack_weight(x_words, x_scales)[:, unstriped(two)]
    s = 0.0625 * (d_kidx.T @ x_two)
    top2 = s.max(axis=1, keepdims=True)
    ea2 = np.exp(f64(tau2) * (s[:, unstriped(n2)] - top2))
    sm = s * ea2
    ds = np.zeros((H, S))
    ds[:, unstriped(n3)] = sm
    z2 = f64(gk) * (2.0 * ds - (0.5 * s))
    h = unpack_weight(w2_words, w2_scales).T @ mxq(z, 0, "e4m3") + unpack_weight(w3_words, w3_scales).T @ mxq(z2, 0, "e4m3")
    old = h[:, unstriped(n4)]
    pa = h[:, unstriped(n5)]
    ra = old - (0.5 * pa)
    out = h.copy()
    out[:, unstriped(n4)] = ra
    return (out,) + planes(out)

from contextlib import ExitStack

import concourse.mybir as mybir

F32 = mybir.dt.float32
BF16 = mybir.dt.bfloat16
I32 = mybir.dt.int32
U32 = mybir.dt.uint32
U16 = mybir.dt.uint16
U8 = mybir.dt.uint8
FP8X4 = mybir.dt.float8_e4m3fn_x4
ALU = mybir.AluOpType
ACT = mybir.ActivationFunctionType
AX = mybir.AxisListType

P = 128
PACK = 4
K, T, S, N, H, G, W, U = 512, 1024, 256, 512, 512, 2048, 1024, 192
FLOPS = 4 * 2 * 512 * 512 * 256


def tile_picked_jkeyeglesdkdif_none_po_kernel(
    tc, x_words, x_scales, w1_words, w1_scales, d_words, d_scales, tau, tau2, gn, gk,
    w2_words, w2_scales, w3_words, w3_scales, offs, kidx, two, n1, n2, n3, n4, n5,
    out_0, out_1, out_2,
):
    nc = tc.nc
    with ExitStack() as ctx:
        sb = ctx.enter_context(tc.tile_pool(name="sb", bufs=1))
        psum = ctx.enter_context(tc.psum_pool(name="psum", bufs=1))

        def tile(name, cols, dtype):
            return sb.tile([P, cols], dtype, name=name, align_bytes=64)

        def load_list(name, src):
            t = sb.tile([P, src.shape[1]], U16, name=name)
            nc.sync.dma_start(t[:], src)
            return t

        def load_words(queue, name, src):
            t = tile(name, src.shape[2], U32)
            queue.dma_start(t[:].bitcast(I32), src[0].rearrange("p n t -> p (n t)").bitcast(I32))
            return t

        def zeroed(name, cols):
            t = tile(name, cols, U8)
            nc.vector.memset(t[:].bitcast(I32), 0)
            return t

        def load_scales(queue, t, src, first):
            for r in range(4):
                queue.dma_start(t[first + r : P : 32, :].bitcast(I32), src[0, r:16:4, :].bitcast(I32))

        def load_scales_filled(name, src, rows):
            t = tile(name, src.shape[2], U8)
            for q in rows:
                quad = src[0, 4 * q : 4 * q + 4, :].bitcast(I32)
                nc.sync.dma_start(t[32 * q : 32 * q + 32, :].bitcast(I32), quad.unsqueeze(0).to_broadcast([8, 4, src.shape[2] // 4]))
            return t

        def fill_scales(t, src, q):
            quad = src[0, 4 * q : 4 * q + 4, :].bitcast(I32)
            nc.sync.dma_start(t[32 * q : 32 * q + 32, :].bitcast(I32), quad.unsqueeze(0).to_broadcast([8, 4, src.shape[2] // 4]))

        def load_column(queue, name, src):
            t = tile(name, PACK, F32)
            queue.dma_start(t[:], src.rearrange("(p t) o -> p (t o)", t=PACK))
            return t

        def deal(copy, name, src):
            t = tile(name, H, src.dtype)
            copy(t[:].rearrange("p (t m) -> p m t", t=PACK), src[:].rearrange("p (m t) -> p m t", t=PACK))
            return t

        def gather(name, cols, table, offsets):
            t = tile(name, cols, table.dtype)
            nc.vector.tensor_copy(t[:], table[:].indirect(offsets[:]))
            return t

        def product(bank, words, scales, first, t, rhs_words, rhs_scales, start, stop):
            cols = slice(P * t, P * (t + 1))
            nc.tensor.matmul_mx(
                out=bank[:, 0:S], lhsT=words[:, cols].bitcast(FP8X4), lhsT_scale=scales[first:P, cols],
                rhs=rhs_words[:].bitcast(FP8X4), rhs_scale=rhs_scales[:], start=start, stop=stop)

        dsc = zeroed("dsc", G)
        w23s = zeroed("w23s", N)
        ks_plane = zeroed("ks_plane", H)
        xs = tile("xs", T, U8)
        w1s = tile("w1s", H, U8)

        offs_t = load_list("offs_t", offs)
        fill_scales(xs, x_scales, 0)
        fill_scales(xs, x_scales, 1)
        tau_t = load_column(nc.sync, "tau_t", tau)
        xw = load_words(nc.sync, "xw", x_words)
        w1w = load_words(nc.sync, "w1w", w1_words)
        fill_scales(xs, x_scales, 2)
        fill_scales(xs, x_scales, 3)
        for q in range(4):
            fill_scales(w1s, w1_scales, q)
        n1_t = load_list("n1_t", n1)
        kidx_t = load_list("kidx_t", kidx)
        for i in range(2):
            nc.sync.dma_start(dsc[i:P:16, :].bitcast(I32), d_scales[0, i:16:2, :].bitcast(I32))
        dw = load_words(nc.sync, "dw", d_words)
        two_t = load_list("two_t", two)
        tau2_t = load_column(nc.sync, "tau2_t", tau2)
        n2_t = load_list("n2_t", n2)
        gk_t = load_column(nc.sync, "gk_t", gk)
        gn_t = load_column(nc.sync, "gn_t", gn)
        n3_t = load_list("n3_t", n3)
        w2w = load_words(nc.sync, "w2w", w2_words)
        w3w = load_words(nc.sync, "w3w", w3_words)
        load_scales(nc.sync, w23s, w2_scales, 0)
        load_scales(nc.sync, w23s, w3_scales, 4)
        n4_t = load_list("n4_t", n4)
        n5_t = load_list("n5_t", n5)

        ntau = tile("ntau", PACK, F32)
        nc.scalar.activation(ntau[:], tau_t[:], ACT.Copy, scale=-1.0)
        xgs = gather("xgs", S, xs, offs_t)
        xgw = gather("xgw", S, xw, offs_t)
        w1wd = deal(nc.vector.tensor_copy, "w1wd", w1w)
        w1sd = deal(nc.vector.tensor_copy, "w1sd", w1s)

        banks = [psum.tile([P, 512], F32, name=f"bank{b}") for b in range(8)]
        top = tile("top", PACK, F32)
        bias = tile("bias", PACK, F32)
        y = [tile(f"y{t}", 2 * W, F32) for t in range(PACK)]
        ea = [tile(f"ea{t}", W, F32) for t in range(PACK)]
        for t in range(PACK):
            product(banks[t], w1wd, w1sd, 0, t, xgw, xgs, True, True)
        for t in range(PACK):
            col = slice(t, t + 1)
            nc.vector.tensor_scalar(y[t][:, 0:S], banks[t][:, 0:S], 1.0, None, ALU.mult, ALU.max, accum_out=top[:, col])
            nc.vector.tensor_tensor(bias[:, col], top[:, col], ntau[:, col], ALU.mult)
            nc.scalar.activation(ea[t][:], y[t][:].indirect(n1_t[:]), ACT.Exp, bias=bias[:, col], scale=tau_t[:, col])

        kgs = gather("kgs", H, dsc, kidx_t)
        ksd = deal(nc.vector.tensor_copy, "ksd", kgs)
        for r in range(4):
            src = 16 * (r // 2) + r % 2
            nc.sync.dma_start(ks_plane[r:P:32, :].bitcast(I32), ksd[src:P:32, :].bitcast(I32))
        x2s = gather("x2s", S, xs, two_t)
        x2w = gather("x2w", S, xw, two_t)
        kgw = gather("kgw", H, dw, kidx_t)
        kwd = deal(nc.vector.tensor_copy, "kwd", kgw)

        ms = tile("ms", W, F32)
        top2 = [ms[:, c : c + 1] for c in (S, 2 * S, 3 * S, 3 * S + 8)]
        bias2 = tile("bias2", PACK, F32)
        s = [tile(f"s{t}", 2 * S, F32) for t in range(PACK)]
        ea2 = [tile(f"ea2{t}", S, F32) for t in range(PACK)]
        for t in range(PACK):
            product(banks[PACK + t], kwd, ks_plane, 0, t, x2w, x2s, True, True)
        for t in range(PACK):
            col = slice(t, t + 1)
            nc.vector.tensor_scalar(s[t][:, 0:S], banks[PACK + t][:, 0:S], 0.0625, None, ALU.mult, ALU.max, accum_out=top2[t])
            nc.vector.tensor_scalar(bias2[:, col], top2[t], tau2_t[:, col], -1.0, ALU.mult, ALU.mult)
            nc.scalar.activation(ea2[t][:], s[t][:].indirect(n2_t[:]), ACT.Exp, bias=bias2[:, col], scale=tau2_t[:, col])

        for t in range(PACK):
            nc.vector.tensor_reduce(ms[:, S * t : S * (t + 1)], ea[t][:].rearrange("p (j m) -> p j m", m=4), AX.X, ALU.add)
        lg = tile("lg", W, F32)
        nc.scalar.activation(lg[:], ms[:], ACT.Ln, bias=0.25)

        gk2 = tile("gk2", PACK, F32)
        gkh = tile("gkh", PACK, F32)
        nc.vector.tensor_scalar(gk2[:], gk_t[:], 2.0, None, ALU.mult)
        nc.vector.tensor_scalar(gkh[:], gk_t[:], -0.5, None, ALU.mult)
        sm = [tile(f"sm{t}", S, F32) for t in range(PACK)]
        ds = [tile(f"ds{t}", 2 * S, F32) for t in range(PACK)]
        for t in range(PACK):
            nc.vector.scalar_tensor_tensor(sm[t][:], s[t][:, 0:S], gk2[:, t : t + 1], ea2[t][:], ALU.mult, ALU.mult)
            nc.scalar.activation(ds[t][:].indirect(n3_t[:]), sm[t][:], ACT.Copy)

        w2wd = deal(nc.vector.tensor_copy, "w2wd", w2w)
        w3wd = deal(nc.vector.tensor_copy, "w3wd", w3w)
        w23sd = deal(nc.vector.tensor_copy, "w23sd", w23s)

        zf = tile("zf", W, F32)
        zb = tile("zb", W, BF16)
        zb_t = zb[:].rearrange("p (j t) -> p t j", t=PACK)
        for t in range(PACK):
            cols = slice(S * t, S * (t + 1))
            nc.vector.scalar_tensor_tensor(zf[:, cols], y[t][:, 0:S], -0.5, lg[:, cols], ALU.mult, ALU.add)
        for t in range(PACK):
            cols = slice(S * t, S * (t + 1))
            nc.vector.tensor_scalar(zb_t[:, t, :], zf[:, cols], gn_t[:, t : t + 1], None, ALU.mult)
        zw = tile("zw", S, U32)
        zs = tile("zs", S, U8)
        nc.vector.quantize_mx(out=zw[:].bitcast(FP8X4), scales=zs[:], in_=zb[:])
        for t in range(PACK):
            product(banks[t], w2wd, w23sd, 0, t, zw, zs, True, False)

        z2b = tile("z2b", W, BF16)
        z2b_t = z2b[:].rearrange("p (j t) -> p t j", t=PACK)
        for t in range(PACK):
            nc.vector.scalar_tensor_tensor(z2b_t[:, t, :], s[t][:, 0:S], gkh[:, t : t + 1], ds[t][:, 0:S], ALU.mult, ALU.add)
        z2w = tile("z2w", S, U32)
        z2s = tile("z2s", S, U8)
        nc.vector.quantize_mx(out=z2w[:].bitcast(FP8X4), scales=z2s[:], in_=z2b[:])
        for t in range(PACK):
            product(banks[t], w3wd, w23sd, 4, t, z2w, z2s, False, True)

        ob = tile("ob", W, BF16)
        ob_t = ob[:].rearrange("p (j t) -> p t j", t=PACK)
        out_rows = out_0.rearrange("(p t) j -> p t j", t=PACK)
        o = [tile(f"o{t}", S, F32) for t in range(PACK)]
        old = [tile(f"old{t}", U, F32) for t in range(PACK)]
        pa = [tile(f"pa{t}", U, F32) for t in range(PACK)]
        ra = [tile(f"ra{t}", U, F32) for t in range(PACK)]
        for t in range(PACK):
            nc.vector.tensor_copy(o[t][:], banks[t][:, 0:S])
        for t in range(PACK):
            nc.scalar.activation(old[t][:], o[t][:].indirect(n4_t[:]), ACT.Copy)
            nc.scalar.activation(pa[t][:], o[t][:].indirect(n5_t[:]), ACT.Copy)
            nc.vector.scalar_tensor_tensor(ra[t][:], pa[t][:], -0.5, old[t][:], ALU.mult, ALU.add)
        for t in range(PACK):
            nc.scalar.activation(o[t][:].indirect(n4_t[:]), ra[t][:], ACT.Copy)
            nc.sync.dma_start(out_rows[:, t, :], o[t][:])
            nc.vector.tensor_copy(ob_t[:, t, :], o[t][:])
        ow = tile("ow", S, U32)
        osc = tile("osc", S, U8)
        nc.vector.quantize_mx(out=ow[:].bitcast(FP8X4), scales=osc[:], in_=ob[:])
        nc.sync.dma_start(out_1[0].rearrange("p n t -> p (n t)").bitcast(I32), ow[:].bitcast(I32))
        for q in range(4):
            queue = nc.scalar if q % 2 else nc.sync
            queue.dma_start(out_2[0, 4 * q : 4 * q + 4, :].bitcast(I32), osc[32 * q : 32 * q + 4, :].bitcast(I32))
